import numpy as np
import ml_dtypes


def mxq(x, axis, fmt="e4m3"):
    dtype, down = {"e4m3": (ml_dtypes.float8_e4m3fn, 7), "e5m2": (ml_dtypes.float8_e5m2, 14)}[fmt]
    v = np.moveaxis(np.asarray(x, np.float32).astype(ml_dtypes.bfloat16).astype(np.float64), axis, -1)
    blocks = v.reshape(v.shape[:-1] + (-1, 32))
    amax = np.abs(blocks).max(-1, keepdims=True)
    byte = np.maximum(np.where(amax > 0, np.frexp(amax)[1] - 1 + 127, 0) - down, 1)
    scale = np.exp2(byte - 127.0)
    codes = (blocks / scale).astype(np.float32).astype(dtype).astype(np.float64)
    return np.moveaxis((codes * scale).reshape(v.shape), -1, axis)


WIDE = False


def mx_kscale(k):
    if not WIDE:
        return np.ones(k)
    levels = np.array([10, -10, 5, -5, 0])
    if k % 512:
        return np.exp2(np.random.permutation(np.resize(levels, k // 32))).repeat(32)
    a = np.empty((k // 512, 16))
    for p in range(k // 512):
        a[p, :8] = np.random.permutation(np.resize(levels, 8))
        for g in range(8):
            far = levels[np.abs(levels - a[p, g]) >= 10]
            a[p, g + 8] = far[np.random.randint(len(far))]
    return np.exp2(a.ravel()).repeat(32)


def f64(x):
    return np.asarray(x).astype(np.float64)


def striped(idx):
    return np.tile(np.asarray(idx).reshape(-1, 16).T, (8, 1)).astype(np.uint16)


def unstriped(offs):
    return offs[:16].T.reshape(-1).astype(np.int64)


E2M1 = np.array([0.0, 0.5, 1.0, 1.5, 2.0, 3.0, 4.0, 6.0, -0.0, -0.5, -1.0, -1.5, -2.0, -3.0, -4.0, -6.0])


def pack_weight(w, fmt):
    k, n = w.shape
    w = f64(np.asarray(w, np.float32).astype(ml_dtypes.bfloat16)).reshape(k // 32, 32, n)
    amax = np.abs(w).max(1)
    if fmt == "e4m3":
        byte = np.frexp(amax)[1] - 1 + 127 - 7
    else:
        mant, ex = np.frexp(amax / 6.0)
        byte = np.where(mant > 0.5, ex, ex - 1) + 127
    byte = np.clip(np.where(amax > 0, byte, 1), 1, 254)
    scaled = (w * np.exp2(127.0 - byte)[:, None, :]).reshape(k, n).astype(np.float32)
    by_word = np.ascontiguousarray(scaled.reshape(k // 512, 128, 4, n).transpose(0, 1, 3, 2))
    if fmt == "e4m3":
        words = by_word.astype(ml_dtypes.float8_e4m3fn).view(np.uint8)
    else:
        c = by_word.astype(ml_dtypes.float4_e2m1fn).view(np.uint8) & 0xF
        words = (c[..., 0::2] | (c[..., 1::2] << 4)).reshape(k // 512, 128, 2 * n)
    return np.ascontiguousarray(words), np.ascontiguousarray(byte.astype(np.uint8).reshape(k // 512, 16, n))


def unpack_weight(words, scales, fmt):
    g, _, n = scales.shape
    words = np.ascontiguousarray(words).reshape(g, 128, n, -1)
    if fmt == "e4m3":
        vals = words.view(ml_dtypes.float8_e4m3fn).astype(np.float64)
    else:
        nib = np.empty((g, 128, n, 4), np.uint8)
        nib[..., 0::2] = words & 0xF
        nib[..., 1::2] = words >> 4
        vals = E2M1[nib]
    vals = vals * np.repeat(np.exp2(scales.astype(np.float64) - 127.0), 8, axis=1)[..., None]
    return vals.transpose(0, 1, 3, 2).reshape(g * 512, n)


D, E, T, I, G, U, Q = 512, 512, 4096, 1024, 64, 512, 128


def setup_inputs():
    n = np.random.standard_normal
    idx = np.random.permutation(T)[:I]
    idx2 = np.random.permutation(U)[:G]
    fd = mx_kscale(D)
    fe = mx_kscale(E)
    keysp = pack_weight(n((D, T)) / fd[:, None], "e2m1")
    valsp = pack_weight(n((E, T)) / fe[:, None], "e2m1")
    return {
        "query": (n((D, Q)) * 0.7 / np.sqrt(D) * fd[:, None]).astype(np.float32),
        "keys_words": keysp[0],
        "keys_scales": keysp[1],
        "ptab": (n((Q, U)) * 0.4).astype(np.float32),
        "gout": (n((E, Q)) * 1 / np.sqrt(E) * fe[:, None]).astype(np.float32),
        "vals_words": valsp[0],
        "vals_scales": valsp[1],
        "old": (0.5 * n((Q, U))).astype(np.float32),
        "offs": striped(idx),
        "offs2": striped(idx2),
    }


def reference(query, keys_words, keys_scales, ptab, gout, vals_words, vals_scales, old, offs, offs2):
    idx = unstriped(offs)
    idx2 = unstriped(offs2)
    keysu = unpack_weight(keys_words, keys_scales, "e2m1")
    valsu = unpack_weight(vals_words, vals_scales, "e2m1")
    queryq = mxq(f64(query), 0, "e4m3")
    keysidxg = keysu[:, idx]
    a = queryq.T @ keysidxg
    tp = np.exp(f64(ptab)[:, idx2])
    tr1 = np.repeat(tp, I // G, axis=1)
    s = a * tr1
    p = np.exp(s - np.max(s, axis=1, keepdims=True))
    z = np.sum(p, axis=1, keepdims=True)
    goutq = mxq(f64(gout), 0, "e4m3")
    valsidxg = valsu[:, idx]
    c0 = goutq.T @ valsidxg
    dz = np.sum(p * c0, axis=1, keepdims=True) / np.square(z) * (-1.0)
    dp = 1.0 / z * c0 + dz
    ds = dp * p
    dtr1 = ds * a
    dtp = dtr1.reshape(Q, G, I // G).sum(axis=2)
    gs = dtp * tp * 64.0
    gf = np.zeros((Q, U))
    gf[:, idx2] = gs
    y = f64(old) + gf
    return y

@@ -1,0 +1,170 @@
+from contextlib import ExitStack
+
+import concourse.mybir as mybir
+
+D, T, I, G, U, Q = 512, 4096, 1024, 64, 512, 128
+P = 128
+PACK = 4
+PAGE = I // G
+HALF = 512
+HALVES = I // HALF
+PAGES_HALF = HALF // PAGE
+LIST_COLS_HALF = HALF // 16
+
+F32 = mybir.dt.float32
+BF16 = mybir.dt.bfloat16
+I32 = mybir.dt.int32
+U32 = mybir.dt.uint32
+U16 = mybir.dt.uint16
+U8 = mybir.dt.uint8
+FP8X4 = mybir.dt.float8_e4m3fn_x4
+FP4X4 = mybir.dt.float4_e2m1fn_x4
+ALU = mybir.AluOpType
+ACT = mybir.ActivationFunctionType
+AX = mybir.AxisListType
+
+FLOPS = 2 * 2 * D * Q * I
+
+
+def load_scale_rows(nc, plane, scales):
+    rows = scales[0].rearrange("(quad r) c -> r quad c", r=4)
+    for r in range(4):
+        nc.sync.dma_start(out=plane[r:P:32, :].bitcast(I32), in_=rows[r].bitcast(I32))
+
+
+def tile_attend_bpagetemper_kernel(tc, query, keys_words, keys_scales, ptab, gout, vals_words, vals_scales, old, offs, offs2, out):
+    nc = tc.nc
+    with ExitStack() as ctx:
+        held = ctx.enter_context(tc.tile_pool(name="held", bufs=1))
+        work = ctx.enter_context(tc.tile_pool(name="work", bufs=1))
+        psum = ctx.enter_context(tc.psum_pool(name="psum", bufs=1))
+
+        slots = held.tile([P, I // 16], U16, name="slots")
+        pages = held.tile([P, G // 16], U16, name="pages")
+        k_scales = work.tile([P, T], U8, name="k_scales", tag="ks_then_old", align_bytes=64)
+        q_raw = work.tile([P, PACK, Q], F32, name="q_raw", tag="q_then_vs", align_bytes=64)
+        ptab_sb = work.tile([P, U], F32, name="ptab_sb", tag="ptab_then_kw", align_bytes=64)
+        gf = held.tile([P, U], F32, name="gf")
+
+        nc.vector.memset(k_scales[:].bitcast(I32), 0)
+        nc.vector.memset(gf[:], 0.0)
+
+        nc.sync.dma_start(pages[:], offs2)
+        nc.sync.dma_start(out=ptab_sb[:], in_=ptab)
+        nc.sync.dma_start(slots[:], offs)
+        nc.sync.dma_start(out=q_raw[:], in_=query.rearrange("(p j) w -> p j w", j=PACK))
+        load_scale_rows(nc, k_scales, keys_scales)
+
+        ptab_g = work.tile([P, G], F32, name="ptab_g", tag="ptabg_then_g")
+        tp = work.tile([P, G], F32, name="tp")
+        nc.vector.tensor_copy(out=ptab_g[:], in_=ptab_sb[:].indirect(pages[:]))
+        nc.scalar.activation(out=tp[:], in_=ptab_g[:], func=ACT.Exp)
+        k_words = work.tile([P, T], U16, name="k_words", tag="ptab_then_kw", align_bytes=64)
+        nc.sync.dma_start(out=k_words[:].bitcast(I32), in_=keys_words[0].bitcast(I32))
+        g_raw = work.tile([P, PACK, Q], F32, name="g_raw", tag="ptabg_then_g")
+        nc.sync.dma_start(out=g_raw[:], in_=gout.rearrange("(p j) w -> p j w", j=PACK))
+
+        q_grouped = work.tile([P, Q, PACK], BF16, name="q_grouped", tag="qg_then_vw", align_bytes=64)
+        q_codes = work.tile([P, Q], U32, name="q_codes", align_bytes=64)
+        q_scales = work.tile([P, Q], U8, name="q_scales", align_bytes=64)
+        nc.vector.tensor_copy(out=q_grouped[:], in_=q_raw[:].rearrange("p j w -> p w j"))
+        v_scales = work.tile([P, T], U8, name="v_scales", tag="q_then_vs", align_bytes=64)
+        nc.vector.memset(v_scales[:].bitcast(I32), 0)
+        load_scale_rows(nc, v_scales, vals_scales)
+        nc.vector.quantize_mx(out=q_codes[:].bitcast(FP8X4), scales=q_scales[:], in_=q_grouped[:].rearrange("p w j -> p (w j)"))
+        v_words = work.tile([P, T], U16, name="v_words", tag="qg_then_vw", align_bytes=64)
+        nc.sync.dma_start(out=v_words[:].bitcast(I32), in_=vals_words[0].bitcast(I32))
+
+        def list_half(h):
+            return slots[:, h * LIST_COLS_HALF : (h + 1) * LIST_COLS_HALF]
+
+        def cols(h):
+            return slice(h * HALF, (h + 1) * HALF)
+
+        kg_scales = work.tile([P, I], U8, name="kg_scales", align_bytes=64)
+        nc.vector.tensor_copy(out=kg_scales[:], in_=k_scales[:].indirect(slots[:]))
+
+        old_sb = work.tile([P, U], F32, name="old_sb", tag="ks_then_old", align_bytes=64)
+        nc.sync.dma_start(out=old_sb[:], in_=old)
+
+        a_ps = []
+        for h in range(HALVES):
+            kg_words = work.tile([P, HALF], U16, name=f"kg_words{h}", align_bytes=64)
+            nc.vector.tensor_copy(out=kg_words[:], in_=k_words[:].indirect(list_half(h)))
+            bank = psum.tile([P, HALF], F32, name=f"a{h}")
+            nc.tensor.matmul_mx(out=bank[:], lhsT=q_codes[:].bitcast(FP8X4), lhsT_scale=q_scales[:],
+                                rhs=kg_words[:].bitcast(FP4X4), rhs_scale=kg_scales[:, cols(h)], start=True, stop=True)
+            a_ps.append(bank)
+
+        g_grouped = work.tile([P, Q, PACK], BF16, name="g_grouped", align_bytes=64)
+        g_codes = work.tile([P, Q], U32, name="g_codes", align_bytes=64)
+        g_scales = work.tile([P, Q], U8, name="g_scales", align_bytes=64)
+        nc.scalar.copy(out=g_grouped[:], in_=g_raw[:].rearrange("p j w -> p w j"))
+
+        s = work.tile([P, I], F32, name="s")
+        vg_scales = []
+        for h in range(HALVES):
+            nc.vector.tensor_tensor(
+                out=s[:, cols(h)].rearrange("p (g j) -> p g j", j=PAGE),
+                in0=a_ps[h][:].rearrange("p (g j) -> p g j", j=PAGE),
+                in1=tp[:, h * PAGES_HALF : (h + 1) * PAGES_HALF].unsqueeze(2).to_broadcast([P, PAGES_HALF, PAGE]),
+                op=ALU.mult)
+            vgs = work.tile([P, HALF], U8, name=f"vg_scales{h}", tag=f"after_c{h}_a", align_bytes=64)
+            nc.vector.tensor_copy(out=vgs[:], in_=v_scales[:].indirect(list_half(h)))
+            vg_scales.append(vgs)
+        neg_max = work.tile([P, 1], F32, name="neg_max")
+        nc.vector.tensor_reduce(out=neg_max[:], in_=s[:], axis=AX.X, op=ALU.max, negate=True)
+        nc.vector.quantize_mx(out=g_codes[:].bitcast(FP8X4), scales=g_scales[:], in_=g_grouped[:].rearrange("p w j -> p (w j)"))
+
+        p = work.tile([P, I], F32, name="p")
+        z = work.tile([P, 1], F32, name="z")
+        nc.scalar.activation(out=p[:], in_=s[:], func=ACT.Exp, bias=neg_max[:], accum_out=z[:])
+
+        c_ps = []
+        for h in range(HALVES):
+            vg_words = work.tile([P, HALF], U16, name=f"vg_words{h}", tag=f"after_c{h}_b", align_bytes=64)
+            nc.vector.tensor_copy(out=vg_words[:], in_=v_words[:].indirect(list_half(h)))
+            bank = psum.tile([P, HALF], F32, name=f"c{h}")
+            nc.tensor.matmul_mx(out=bank[:], lhsT=g_codes[:].bitcast(FP8X4), lhsT_scale=g_scales[:],
+                                rhs=vg_words[:].bitcast(FP4X4), rhs_scale=vg_scales[h][:], start=True, stop=True)
+            c_ps.append(bank)
+
+        pc = work.tile([P, I], F32, name="pc")
+        pc_sums = [work.tile([P, 1], F32, name=f"pc_sum{h}") for h in range(HALVES)]
+
+        def weigh(h):
+            nc.vector.scalar_tensor_tensor(out=pc[:, cols(h)], in0=c_ps[h][:], scalar=1.0, in1=p[:, cols(h)],
+                                           op0=ALU.mult, op1=ALU.mult, accum_out=pc_sums[h][:])
+
+        sp0 = work.tile([P, HALF], F32, name="sp0", tag="after_c0_b", align_bytes=64)
+        weigh(0)
+        nc.vector.tensor_tensor(out=sp0[:], in0=s[:, cols(0)], in1=p[:, cols(0)], op=ALU.mult)
+        weigh(1)
+        rz = work.tile([P, 1], F32, name="rz", tag="after_c1_a", align_bytes=64)
+        nc.vector.reciprocal(out=rz[:], in_=z[:])
+        sp1 = work.tile([P, HALF], F32, name="sp1", tag="after_c1_b", align_bytes=64)
+        QH = HALF // 2
+        nc.vector.tensor_tensor(out=sp1[:, :QH], in0=s[:, HALF : HALF + QH], in1=p[:, HALF : HALF + QH], op=ALU.mult)
+        mean_c = work.tile([P, 1], F32, name="mean_c")
+        nc.vector.tensor_scalar(out=mean_c[:], in0=pc_sums[0][:], scalar1=pc_sums[1][:], scalar2=rz[:], op0=ALU.add, op1=ALU.mult)
+        nc.vector.tensor_tensor(out=sp1[:, QH:], in0=s[:, HALF + QH :], in1=p[:, HALF + QH :], op=ALU.mult)
+
+        sixty_four = work.tile([P, G], F32, name="sixty_four")
+        factor = work.tile([P, G], F32, name="factor")
+        nc.vector.memset(sixty_four[:], 64.0)
+        nc.scalar.activation(out=factor[:], in_=sixty_four[:], func=ACT.Copy, scale=rz[:])
+
+        w = work.tile([P, I], F32, name="w")
+        page_sums = work.tile([P, G], F32, name="page_sums")
+        for h, sp in enumerate((sp0, sp1)):
+            nc.vector.scalar_tensor_tensor(out=w[:, cols(h)], in0=c_ps[h][:], scalar=mean_c[:], in1=sp[:],
+                                           op0=ALU.subtract, op1=ALU.mult)
+        for h in range(HALVES):
+            nc.vector.tensor_reduce(out=page_sums[:, h * PAGES_HALF : (h + 1) * PAGES_HALF],
+                                    in_=w[:, cols(h)].rearrange("p (g j) -> p g j", j=PAGE), axis=AX.X, op=ALU.add)
+        nc.vector.tensor_tensor(out=gf[:].indirect(pages[:]), in0=page_sums[:], in1=factor[:], op=ALU.mult)
+        result = work.tile([P, U], F32, name="result")
+        for h in range(2):
+            half = slice(h * U // 2, (h + 1) * U // 2)
+            nc.vector.tensor_tensor(out=result[:, half], in0=gf[:, half], in1=old_sb[:, half], op=ALU.add)
+            nc.sync.dma_start(out=out[:, half], in_=result[:, half])

@@ -42,36 +42,39 @@ def tile_attend_bpagetemper_kernel(tc, query, keys_words, keys_scales, ptab, gou
         slots = held.tile([P, I // 16], U16, name="slots")
         pages = held.tile([P, G // 16], U16, name="pages")
         k_scales = work.tile([P, T], U8, name="k_scales", tag="ks_then_old", align_bytes=64)
-        q_raw = work.tile([P, PACK, Q], F32, name="q_raw", tag="q_then_vs", align_bytes=64)
-        ptab_sb = work.tile([P, U], F32, name="ptab_sb", tag="ptab_then_kw", align_bytes=64)
+        q_raw = work.tile([P, PACK, Q], F32, name="q_raw", tag="q_then_g", align_bytes=64)
+        ptab_sb = work.tile([P, U], F32, name="ptab_sb", align_bytes=64)
         gf = held.tile([P, U], F32, name="gf")
 
+        k_words = work.tile([P, T], U16, name="k_words", align_bytes=64)
+        q_grouped = work.tile([P, Q, PACK], BF16, name="q_grouped", tag="qg_then_vw", align_bytes=64)
+        v_scales = work.tile([P, T], U8, name="v_scales", tag="vs_then_max", align_bytes=64)
+        sixty_four = work.tile([P, G], F32, name="sixty_four")
+
         nc.vector.memset(k_scales[:].bitcast(I32), 0)
+        nc.vector.memset(v_scales[:].bitcast(I32), 0)
         nc.vector.memset(gf[:], 0.0)
+        nc.vector.memset(sixty_four[:], 64.0)
 
         nc.sync.dma_start(pages[:], offs2)
         nc.sync.dma_start(out=ptab_sb[:], in_=ptab)
         nc.sync.dma_start(slots[:], offs)
         nc.sync.dma_start(out=q_raw[:], in_=query.rearrange("(p j) w -> p j w", j=PACK))
         load_scale_rows(nc, k_scales, keys_scales)
+        nc.sync.dma_start(out=k_words[:].bitcast(I32), in_=keys_words[0].bitcast(I32))
+        load_scale_rows(nc, v_scales, vals_scales)
 
-        ptab_g = work.tile([P, G], F32, name="ptab_g", tag="ptabg_then_g")
+        ptab_g = work.tile([P, G], F32, name="ptab_g")
         tp = work.tile([P, G], F32, name="tp")
         nc.vector.tensor_copy(out=ptab_g[:], in_=ptab_sb[:].indirect(pages[:]))
         nc.scalar.activation(out=tp[:], in_=ptab_g[:], func=ACT.Exp)
-        k_words = work.tile([P, T], U16, name="k_words", tag="ptab_then_kw", align_bytes=64)
-        nc.sync.dma_start(out=k_words[:].bitcast(I32), in_=keys_words[0].bitcast(I32))
-        g_raw = work.tile([P, PACK, Q], F32, name="g_raw", tag="ptabg_then_g")
-        nc.sync.dma_start(out=g_raw[:], in_=gout.rearrange("(p j) w -> p j w", j=PACK))
 
-        q_grouped = work.tile([P, Q, PACK], BF16, name="q_grouped", tag="qg_then_vw", align_bytes=64)
         q_codes = work.tile([P, Q], U32, name="q_codes", align_bytes=64)
         q_scales = work.tile([P, Q], U8, name="q_scales", align_bytes=64)
         nc.vector.tensor_copy(out=q_grouped[:], in_=q_raw[:].rearrange("p j w -> p w j"))
-        v_scales = work.tile([P, T], U8, name="v_scales", tag="q_then_vs", align_bytes=64)
-        nc.vector.memset(v_scales[:].bitcast(I32), 0)
-        load_scale_rows(nc, v_scales, vals_scales)
         nc.vector.quantize_mx(out=q_codes[:].bitcast(FP8X4), scales=q_scales[:], in_=q_grouped[:].rearrange("p w j -> p (w j)"))
+        g_raw = work.tile([P, PACK, Q], F32, name="g_raw", tag="q_then_g", align_bytes=64)
+        nc.sync.dma_start(out=g_raw[:], in_=gout.rearrange("(p j) w -> p j w", j=PACK))
         v_words = work.tile([P, T], U16, name="v_words", tag="qg_then_vw", align_bytes=64)
         nc.sync.dma_start(out=v_words[:].bitcast(I32), in_=vals_words[0].bitcast(I32))
 
@@ -83,7 +86,6 @@ def tile_attend_bpagetemper_kernel(tc, query, keys_words, keys_scales, ptab, gou
 
         kg_scales = work.tile([P, I], U8, name="kg_scales", align_bytes=64)
         nc.vector.tensor_copy(out=kg_scales[:], in_=k_scales[:].indirect(slots[:]))
-
         old_sb = work.tile([P, U], F32, name="old_sb", tag="ks_then_old", align_bytes=64)
         nc.sync.dma_start(out=old_sb[:], in_=old)
 
@@ -104,21 +106,31 @@ def tile_attend_bpagetemper_kernel(tc, query, keys_words, keys_scales, ptab, gou
         s = work.tile([P, I], F32, name="s")
         vg_scales = []
         for h in range(HALVES):
-            nc.vector.tensor_tensor(
+            a_sb = work.tile([P, HALF], F32, name=f"a_sb{h}")
+            nc.scalar.copy(out=a_sb[:], in_=a_ps[h][:])
+            nc.gpsimd.tensor_tensor(
                 out=s[:, cols(h)].rearrange("p (g j) -> p g j", j=PAGE),
-                in0=a_ps[h][:].rearrange("p (g j) -> p g j", j=PAGE),
+                in0=a_sb[:].rearrange("p (g j) -> p g j", j=PAGE),
                 in1=tp[:, h * PAGES_HALF : (h + 1) * PAGES_HALF].unsqueeze(2).to_broadcast([P, PAGES_HALF, PAGE]),
                 op=ALU.mult)
             vgs = work.tile([P, HALF], U8, name=f"vg_scales{h}", tag=f"after_c{h}_a", align_bytes=64)
             nc.vector.tensor_copy(out=vgs[:], in_=v_scales[:].indirect(list_half(h)))
             vg_scales.append(vgs)
         neg_max = work.tile([P, 1], F32, name="neg_max")
-        nc.vector.tensor_reduce(out=neg_max[:], in_=s[:], axis=AX.X, op=ALU.max, negate=True)
+        neg_max0 = work.tile([P, 1], F32, name="neg_max0", tag="vs_then_max", align_bytes=64)
+        neg_s1 = work.tile([P, HALF], F32, name="neg_s1", tag="after_c1_b", align_bytes=64)
+        nc.vector.tensor_reduce(out=neg_max0[:], in_=s[:, cols(0)], axis=AX.X, op=ALU.max, negate=True)
+        nc.vector.tensor_scalar(out=neg_s1[:], in0=s[:, cols(1)], scalar1=-1.0, scalar2=neg_max0[:], op0=ALU.mult, op1=ALU.min, accum_out=neg_max[:])
         nc.vector.quantize_mx(out=g_codes[:].bitcast(FP8X4), scales=g_scales[:], in_=g_grouped[:].rearrange("p w j -> p (w j)"))
 
         p = work.tile([P, I], F32, name="p")
         z = work.tile([P, 1], F32, name="z")
-        nc.scalar.activation(out=p[:], in_=s[:], func=ACT.Exp, bias=neg_max[:], accum_out=z[:])
+        z_half = [work.tile([P, 1], F32, name=f"z_half{h}") for h in range(HALVES)]
+        sp = work.tile([P, I], F32, name="sp")
+        for h in range(HALVES):
+            nc.scalar.activation(out=p[:, cols(h)], in_=s[:, cols(h)], func=ACT.Exp, bias=neg_max[:], accum_out=z_half[h][:])
+            nc.gpsimd.tensor_tensor(out=sp[:, cols(h)], in0=s[:, cols(h)], in1=p[:, cols(h)], op=ALU.mult)
+        nc.scalar.activation(out=z[:], in_=z_half[0][:], func=ACT.Identity, bias=z_half[1][:])
 
         c_ps = []
         for h in range(HALVES):
@@ -136,28 +148,20 @@ def tile_attend_bpagetemper_kernel(tc, query, keys_words, keys_scales, ptab, gou
             nc.vector.scalar_tensor_tensor(out=pc[:, cols(h)], in0=c_ps[h][:], scalar=1.0, in1=p[:, cols(h)],
                                            op0=ALU.mult, op1=ALU.mult, accum_out=pc_sums[h][:])
 
-        sp0 = work.tile([P, HALF], F32, name="sp0", tag="after_c0_b", align_bytes=64)
         weigh(0)
-        nc.vector.tensor_tensor(out=sp0[:], in0=s[:, cols(0)], in1=p[:, cols(0)], op=ALU.mult)
-        weigh(1)
-        rz = work.tile([P, 1], F32, name="rz", tag="after_c1_a", align_bytes=64)
+        rz = work.tile([P, 1], F32, name="rz", tag="after_c0_a", align_bytes=64)
         nc.vector.reciprocal(out=rz[:], in_=z[:])
-        sp1 = work.tile([P, HALF], F32, name="sp1", tag="after_c1_b", align_bytes=64)
-        QH = HALF // 2
-        nc.vector.tensor_tensor(out=sp1[:, :QH], in0=s[:, HALF : HALF + QH], in1=p[:, HALF : HALF + QH], op=ALU.mult)
+        weigh(1)
         mean_c = work.tile([P, 1], F32, name="mean_c")
         nc.vector.tensor_scalar(out=mean_c[:], in0=pc_sums[0][:], scalar1=pc_sums[1][:], scalar2=rz[:], op0=ALU.add, op1=ALU.mult)
-        nc.vector.tensor_tensor(out=sp1[:, QH:], in0=s[:, HALF + QH :], in1=p[:, HALF + QH :], op=ALU.mult)
 
-        sixty_four = work.tile([P, G], F32, name="sixty_four")
         factor = work.tile([P, G], F32, name="factor")
-        nc.vector.memset(sixty_four[:], 64.0)
         nc.scalar.activation(out=factor[:], in_=sixty_four[:], func=ACT.Copy, scale=rz[:])
 
         w = work.tile([P, I], F32, name="w")
         page_sums = work.tile([P, G], F32, name="page_sums")
-        for h, sp in enumerate((sp0, sp1)):
-            nc.vector.scalar_tensor_tensor(out=w[:, cols(h)], in0=c_ps[h][:], scalar=mean_c[:], in1=sp[:],
+        for h in range(HALVES):
+            nc.vector.scalar_tensor_tensor(out=w[:, cols(h)], in0=c_ps[h][:], scalar=mean_c[:], in1=sp[:, cols(h)],
                                            op0=ALU.subtract, op1=ALU.mult)
         for h in range(HALVES):
             nc.vector.tensor_reduce(out=page_sums[:, h * PAGES_HALF : (h + 1) * PAGES_HALF],

@@ -48,22 +48,24 @@ def tile_attend_bpagetemper_kernel(tc, query, keys_words, keys_scales, ptab, gou
 
         k_words = work.tile([P, T], U16, name="k_words", align_bytes=64)
         q_grouped = work.tile([P, Q, PACK], BF16, name="q_grouped", tag="qg_then_vw", align_bytes=64)
-        v_scales = work.tile([P, T], U8, name="v_scales", tag="vs_then_max", align_bytes=64)
+        v_scales = work.tile([P, T], U8, name="v_scales", align_bytes=64)
         sixty_four = work.tile([P, G], F32, name="sixty_four")
 
         nc.vector.memset(k_scales[:].bitcast(I32), 0)
         nc.vector.memset(v_scales[:].bitcast(I32), 0)
         nc.vector.memset(gf[:], 0.0)
-        nc.vector.memset(sixty_four[:], 64.0)
+        nc.vector.memset(sixty_four[:], -64.0)
 
+        nc.sync.dma_start(slots[:], offs)
+        nc.sync.dma_start(out=k_words[:].bitcast(I32), in_=keys_words[0].bitcast(I32))
+        nc.sync.dma_start(out=q_raw[:], in_=query.rearrange("(p j) w -> p j w", j=PACK))
         nc.sync.dma_start(pages[:], offs2)
         nc.sync.dma_start(out=ptab_sb[:], in_=ptab)
-        nc.sync.dma_start(slots[:], offs)
-        nc.sync.dma_start(out=q_raw[:], in_=query.rearrange("(p j) w -> p j w", j=PACK))
         load_scale_rows(nc, k_scales, keys_scales)
-        nc.sync.dma_start(out=k_words[:].bitcast(I32), in_=keys_words[0].bitcast(I32))
         load_scale_rows(nc, v_scales, vals_scales)
 
+        kg_words = work.tile([P, I], U16, name="kg_words", align_bytes=64)
+        nc.vector.tensor_copy(out=kg_words[:], in_=k_words[:].indirect(slots[:]))
         ptab_g = work.tile([P, G], F32, name="ptab_g")
         tp = work.tile([P, G], F32, name="tp")
         nc.vector.tensor_copy(out=ptab_g[:], in_=ptab_sb[:].indirect(pages[:]))
@@ -71,7 +73,7 @@ def tile_attend_bpagetemper_kernel(tc, query, keys_words, keys_scales, ptab, gou
 
         q_codes = work.tile([P, Q], U32, name="q_codes", align_bytes=64)
         q_scales = work.tile([P, Q], U8, name="q_scales", align_bytes=64)
-        nc.vector.tensor_copy(out=q_grouped[:], in_=q_raw[:].rearrange("p j w -> p w j"))
+        nc.scalar.copy(out=q_grouped[:], in_=q_raw[:].rearrange("p j w -> p w j"))
         nc.vector.quantize_mx(out=q_codes[:].bitcast(FP8X4), scales=q_scales[:], in_=q_grouped[:].rearrange("p w j -> p (w j)"))
         g_raw = work.tile([P, PACK, Q], F32, name="g_raw", tag="q_then_g", align_bytes=64)
         nc.sync.dma_start(out=g_raw[:], in_=gout.rearrange("(p j) w -> p j w", j=PACK))
@@ -84,27 +86,23 @@ def tile_attend_bpagetemper_kernel(tc, query, keys_words, keys_scales, ptab, gou
         def cols(h):
             return slice(h * HALF, (h + 1) * HALF)
 
-        kg_scales = work.tile([P, I], U8, name="kg_scales", align_bytes=64)
-        nc.vector.tensor_copy(out=kg_scales[:], in_=k_scales[:].indirect(slots[:]))
+        a_ps = []
+        for h in range(HALVES):
+            kg_scales = work.tile([P, HALF], U8, name=f"kg_scales{h}", align_bytes=64)
+            nc.vector.tensor_copy(out=kg_scales[:], in_=k_scales[:].indirect(list_half(h)))
+            bank = psum.tile([P, HALF], F32, name=f"a{h}")
+            nc.tensor.matmul_mx(out=bank[:], lhsT=q_codes[:].bitcast(FP8X4), lhsT_scale=q_scales[:],
+                                rhs=kg_words[:, cols(h)].bitcast(FP4X4), rhs_scale=kg_scales[:], start=True, stop=True)
+            a_ps.append(bank)
         old_sb = work.tile([P, U], F32, name="old_sb", tag="ks_then_old", align_bytes=64)
         nc.sync.dma_start(out=old_sb[:], in_=old)
 
-        a_ps = []
-        for h in range(HALVES):
-            kg_words = work.tile([P, HALF], U16, name=f"kg_words{h}", align_bytes=64)
-            nc.vector.tensor_copy(out=kg_words[:], in_=k_words[:].indirect(list_half(h)))
-            bank = psum.tile([P, HALF], F32, name=f"a{h}")
-            nc.tensor.matmul_mx(out=bank[:], lhsT=q_codes[:].bitcast(FP8X4), lhsT_scale=q_scales[:],
-                                rhs=kg_words[:].bitcast(FP4X4), rhs_scale=kg_scales[:, cols(h)], start=True, stop=True)
-            a_ps.append(bank)
-
-        g_grouped = work.tile([P, Q, PACK], BF16, name="g_grouped", align_bytes=64)
         g_codes = work.tile([P, Q], U32, name="g_codes", align_bytes=64)
         g_scales = work.tile([P, Q], U8, name="g_scales", align_bytes=64)
-        nc.scalar.copy(out=g_grouped[:], in_=g_raw[:].rearrange("p j w -> p w j"))
 
         s = work.tile([P, I], F32, name="s")
-        vg_scales = []
+        vg_scales = work.tile([P, I], U8, name="vg_scales", align_bytes=64)
+        nc.vector.tensor_copy(out=vg_scales[:], in_=v_scales[:].indirect(slots[:]))
         for h in range(HALVES):
             a_sb = work.tile([P, HALF], F32, name=f"a_sb{h}")
             nc.scalar.copy(out=a_sb[:], in_=a_ps[h][:])
@@ -113,15 +111,14 @@ def tile_attend_bpagetemper_kernel(tc, query, keys_words, keys_scales, ptab, gou
                 in0=a_sb[:].rearrange("p (g j) -> p g j", j=PAGE),
                 in1=tp[:, h * PAGES_HALF : (h + 1) * PAGES_HALF].unsqueeze(2).to_broadcast([P, PAGES_HALF, PAGE]),
                 op=ALU.mult)
-            vgs = work.tile([P, HALF], U8, name=f"vg_scales{h}", tag=f"after_c{h}_a", align_bytes=64)
-            nc.vector.tensor_copy(out=vgs[:], in_=v_scales[:].indirect(list_half(h)))
-            vg_scales.append(vgs)
+        g_grouped = work.tile([P, Q, PACK], BF16, name="g_grouped", align_bytes=64)
+        nc.scalar.copy(out=g_grouped[:], in_=g_raw[:].rearrange("p j w -> p w j"))
         neg_max = work.tile([P, 1], F32, name="neg_max")
-        neg_max0 = work.tile([P, 1], F32, name="neg_max0", tag="vs_then_max", align_bytes=64)
+        neg_max0 = work.tile([P, 1], F32, name="neg_max0", tag="q_then_g", align_bytes=64)
         neg_s1 = work.tile([P, HALF], F32, name="neg_s1", tag="after_c1_b", align_bytes=64)
         nc.vector.tensor_reduce(out=neg_max0[:], in_=s[:, cols(0)], axis=AX.X, op=ALU.max, negate=True)
-        nc.vector.tensor_scalar(out=neg_s1[:], in0=s[:, cols(1)], scalar1=-1.0, scalar2=neg_max0[:], op0=ALU.mult, op1=ALU.min, accum_out=neg_max[:])
         nc.vector.quantize_mx(out=g_codes[:].bitcast(FP8X4), scales=g_scales[:], in_=g_grouped[:].rearrange("p w j -> p (w j)"))
+        nc.vector.tensor_scalar(out=neg_s1[:], in0=s[:, cols(1)], scalar1=-1.0, scalar2=neg_max0[:], op0=ALU.mult, op1=ALU.min, accum_out=neg_max[:])
 
         p = work.tile([P, I], F32, name="p")
         z = work.tile([P, 1], F32, name="z")
@@ -138,31 +135,31 @@ def tile_attend_bpagetemper_kernel(tc, query, keys_words, keys_scales, ptab, gou
             nc.vector.tensor_copy(out=vg_words[:], in_=v_words[:].indirect(list_half(h)))
             bank = psum.tile([P, HALF], F32, name=f"c{h}")
             nc.tensor.matmul_mx(out=bank[:], lhsT=g_codes[:].bitcast(FP8X4), lhsT_scale=g_scales[:],
-                                rhs=vg_words[:].bitcast(FP4X4), rhs_scale=vg_scales[h][:], start=True, stop=True)
+                                rhs=vg_words[:].bitcast(FP4X4), rhs_scale=vg_scales[:, cols(h)], start=True, stop=True)
             c_ps.append(bank)
 
         pc = work.tile([P, I], F32, name="pc")
-        pc_sums = [work.tile([P, 1], F32, name=f"pc_sum{h}") for h in range(HALVES)]
-
-        def weigh(h):
-            nc.vector.scalar_tensor_tensor(out=pc[:, cols(h)], in0=c_ps[h][:], scalar=1.0, in1=p[:, cols(h)],
-                                           op0=ALU.mult, op1=ALU.mult, accum_out=pc_sums[h][:])
-
-        weigh(0)
-        rz = work.tile([P, 1], F32, name="rz", tag="after_c0_a", align_bytes=64)
+        pc_sum0 = work.tile([P, 1], F32, name="pc_sum0")
+        mean0 = work.tile([P, 1], F32, name="mean0")
+        mean1 = work.tile([P, 1], F32, name="mean1")
+        rz = work.tile([P, 1], F32, name="rz", tag="after_c0_b", align_bytes=64)
+        nc.vector.scalar_tensor_tensor(out=pc[:, cols(0)], in0=c_ps[0][:], scalar=1.0, in1=p[:, cols(0)],
+                                       op0=ALU.mult, op1=ALU.mult, accum_out=pc_sum0[:])
         nc.vector.reciprocal(out=rz[:], in_=z[:])
-        weigh(1)
-        mean_c = work.tile([P, 1], F32, name="mean_c")
-        nc.vector.tensor_scalar(out=mean_c[:], in0=pc_sums[0][:], scalar1=pc_sums[1][:], scalar2=rz[:], op0=ALU.add, op1=ALU.mult)
-
+        nc.vector.scalar_tensor_tensor(out=pc[:, cols(1)], in0=c_ps[1][:], scalar=rz[:], in1=p[:, cols(1)],
+                                       op0=ALU.mult, op1=ALU.mult, accum_out=mean1[:])
+        nc.scalar.activation(out=mean0[:], in_=pc_sum0[:], func=ACT.Copy, scale=rz[:])
+        shifted = work.tile([P, I], F32, name="shifted")
+        for h in range(HALVES):
+            nc.scalar.activation(out=shifted[:, cols(h)], in_=c_ps[h][:], func=ACT.Identity, scale=-1.0, bias=mean0[:])
         factor = work.tile([P, G], F32, name="factor")
         nc.scalar.activation(out=factor[:], in_=sixty_four[:], func=ACT.Copy, scale=rz[:])
 
         w = work.tile([P, I], F32, name="w")
         page_sums = work.tile([P, G], F32, name="page_sums")
         for h in range(HALVES):
-            nc.vector.scalar_tensor_tensor(out=w[:, cols(h)], in0=c_ps[h][:], scalar=mean_c[:], in1=sp[:, cols(h)],
-                                           op0=ALU.subtract, op1=ALU.mult)
+            nc.vector.scalar_tensor_tensor(out=w[:, cols(h)], in0=shifted[:, cols(h)], scalar=mean1[:], in1=sp[:, cols(h)],
+                                           op0=ALU.add, op1=ALU.mult)
         for h in range(HALVES):
             nc.vector.tensor_reduce(out=page_sums[:, h * PAGES_HALF : (h + 1) * PAGES_HALF],
                                     in_=w[:, cols(h)].rearrange("p (g j) -> p g j", j=PAGE), axis=AX.X, op=ALU.add)

@@ -41,14 +41,14 @@ def tile_attend_bpagetemper_kernel(tc, query, keys_words, keys_scales, ptab, gou
 
         slots = held.tile([P, I // 16], U16, name="slots")
         pages = held.tile([P, G // 16], U16, name="pages")
-        k_scales = work.tile([P, T], U8, name="k_scales", tag="ks_then_old", align_bytes=64)
-        q_raw = work.tile([P, PACK, Q], F32, name="q_raw", tag="q_then_g", align_bytes=64)
+        k_scales = work.tile([P, T], U8, name="k_scales", align_bytes=64)
+        q_raw = work.tile([P, PACK, Q], F32, name="q_raw", align_bytes=64)
         ptab_sb = work.tile([P, U], F32, name="ptab_sb", align_bytes=64)
         gf = held.tile([P, U], F32, name="gf")
 
         k_words = work.tile([P, T], U16, name="k_words", align_bytes=64)
-        q_grouped = work.tile([P, Q, PACK], BF16, name="q_grouped", tag="qg_then_vw", align_bytes=64)
-        v_scales = work.tile([P, T], U8, name="v_scales", align_bytes=64)
+        q_grouped = work.tile([P, Q, PACK], BF16, name="q_grouped", tag="q_then_g", align_bytes=64)
+        v_scales = work.tile([P, T], U8, name="v_scales", tag="vs_then_old", align_bytes=64)
         sixty_four = work.tile([P, G], F32, name="sixty_four")
 
         nc.vector.memset(k_scales[:].bitcast(I32), 0)
@@ -77,8 +77,6 @@ def tile_attend_bpagetemper_kernel(tc, query, keys_words, keys_scales, ptab, gou
         nc.vector.quantize_mx(out=q_codes[:].bitcast(FP8X4), scales=q_scales[:], in_=q_grouped[:].rearrange("p w j -> p (w j)"))
         g_raw = work.tile([P, PACK, Q], F32, name="g_raw", tag="q_then_g", align_bytes=64)
         nc.sync.dma_start(out=g_raw[:], in_=gout.rearrange("(p j) w -> p j w", j=PACK))
-        v_words = work.tile([P, T], U16, name="v_words", tag="qg_then_vw", align_bytes=64)
-        nc.sync.dma_start(out=v_words[:].bitcast(I32), in_=vals_words[0].bitcast(I32))
 
         def list_half(h):
             return slots[:, h * LIST_COLS_HALF : (h + 1) * LIST_COLS_HALF]
@@ -88,14 +86,14 @@ def tile_attend_bpagetemper_kernel(tc, query, keys_words, keys_scales, ptab, gou
 
         a_ps = []
         for h in range(HALVES):
-            kg_scales = work.tile([P, HALF], U8, name=f"kg_scales{h}", align_bytes=64)
+            kg_scales = work.tile([P, HALF], U8, name=f"kg_scales{h}", tag=f"after_a{h}", align_bytes=64)
             nc.vector.tensor_copy(out=kg_scales[:], in_=k_scales[:].indirect(list_half(h)))
             bank = psum.tile([P, HALF], F32, name=f"a{h}")
             nc.tensor.matmul_mx(out=bank[:], lhsT=q_codes[:].bitcast(FP8X4), lhsT_scale=q_scales[:],
                                 rhs=kg_words[:, cols(h)].bitcast(FP4X4), rhs_scale=kg_scales[:], start=True, stop=True)
             a_ps.append(bank)
-        old_sb = work.tile([P, U], F32, name="old_sb", tag="ks_then_old", align_bytes=64)
-        nc.sync.dma_start(out=old_sb[:], in_=old)
+        v_words = work.tile([P, T], U16, name="v_words", tag="after_a0", align_bytes=64)
+        nc.sync.dma_start(out=v_words[:].bitcast(I32), in_=vals_words[0].bitcast(I32))
 
         g_codes = work.tile([P, Q], U32, name="g_codes", align_bytes=64)
         g_scales = work.tile([P, Q], U8, name="g_scales", align_bytes=64)
@@ -103,6 +101,8 @@ def tile_attend_bpagetemper_kernel(tc, query, keys_words, keys_scales, ptab, gou
         s = work.tile([P, I], F32, name="s")
         vg_scales = work.tile([P, I], U8, name="vg_scales", align_bytes=64)
         nc.vector.tensor_copy(out=vg_scales[:], in_=v_scales[:].indirect(slots[:]))
+        old_sb = work.tile([P, U], F32, name="old_sb", tag="vs_then_old", align_bytes=64)
+        nc.sync.dma_start(out=old_sb[:], in_=old)
         for h in range(HALVES):
             a_sb = work.tile([P, HALF], F32, name=f"a_sb{h}")
             nc.scalar.copy(out=a_sb[:], in_=a_ps[h][:])

@@ -10,6 +10,8 @@ HALF = 512
 HALVES = I // HALF
 PAGES_HALF = HALF // PAGE
 LIST_COLS_HALF = HALF // 16
+GPSIMD_SLOTS = 256
+VECTOR_SLOTS = HALF - GPSIMD_SLOTS
 
 F32 = mybir.dt.float32
 BF16 = mybir.dt.bfloat16
@@ -26,10 +28,35 @@ AX = mybir.AxisListType
 FLOPS = 2 * 2 * D * Q * I
 
 
-def load_scale_rows(nc, plane, scales):
+def load_scale_rows(nc, scale_tile, scales):
     rows = scales[0].rearrange("(quad r) c -> r quad c", r=4)
     for r in range(4):
-        nc.sync.dma_start(out=plane[r:P:32, :].bitcast(I32), in_=rows[r].bitcast(I32))
+        nc.sync.dma_start(out=scale_tile[r:P:32, :].bitcast(I32), in_=rows[r].bitcast(I32))
+
+
+def load_rows_by_four(nc, raw, x):
+    nc.sync.dma_start(out=raw[:], in_=x.rearrange("(p t) w -> p t w", t=PACK))
+
+
+def round_and_group(nc, grouped, raw):
+    nc.scalar.copy(out=grouped[:], in_=raw[:].rearrange("p t w -> p w t"))
+
+
+def quantize(nc, codes, scales, grouped):
+    nc.vector.quantize_mx(out=codes[:].bitcast(FP8X4), scales=scales[:], in_=grouped[:].rearrange("p w t -> p (w t)"))
+
+
+def product(nc, bank, codes, scales, words, word_scales):
+    nc.tensor.matmul_mx(out=bank[:], lhsT=codes[:].bitcast(FP8X4), lhsT_scale=scales[:],
+                        rhs=words.bitcast(FP4X4), rhs_scale=word_scales, start=True, stop=True)
+
+
+def by_page(ap):
+    return ap.rearrange("p (g j) -> p g j", j=PAGE)
+
+
+def cols(h):
+    return slice(h * HALF, (h + 1) * HALF)
 
 
 def tile_attend_bpagetemper_kernel(tc, query, keys_words, keys_scales, ptab, gout, vals_words, vals_scales, old, offs, offs2, out):
@@ -45,20 +72,22 @@ def tile_attend_bpagetemper_kernel(tc, query, keys_words, keys_scales, ptab, gou
         q_raw = work.tile([P, PACK, Q], F32, name="q_raw", align_bytes=64)
         ptab_sb = work.tile([P, U], F32, name="ptab_sb", align_bytes=64)
         gf = held.tile([P, U], F32, name="gf")
-
         k_words = work.tile([P, T], U16, name="k_words", align_bytes=64)
-        q_grouped = work.tile([P, Q, PACK], BF16, name="q_grouped", tag="q_then_g", align_bytes=64)
-        v_scales = work.tile([P, T], U8, name="v_scales", tag="vs_then_old", align_bytes=64)
+        q_grouped = work.tile([P, Q, PACK], BF16, name="q_grouped", tag="staging", align_bytes=64)
+        v_scales = work.tile([P, T], U8, name="v_scales", tag="v_scales_then_old", align_bytes=64)
         sixty_four = work.tile([P, G], F32, name="sixty_four")
+
+        def list_half(h):
+            return slots[:, h * LIST_COLS_HALF : (h + 1) * LIST_COLS_HALF]
 
         nc.vector.memset(k_scales[:].bitcast(I32), 0)
         nc.vector.memset(v_scales[:].bitcast(I32), 0)
         nc.vector.memset(gf[:], 0.0)
-        nc.vector.memset(sixty_four[:], -64.0)
+        nc.vector.memset(sixty_four[:], 64.0)
 
-        nc.sync.dma_start(slots[:], offs)
         nc.sync.dma_start(out=k_words[:].bitcast(I32), in_=keys_words[0].bitcast(I32))
-        nc.sync.dma_start(out=q_raw[:], in_=query.rearrange("(p j) w -> p j w", j=PACK))
+        nc.sync.dma_start(slots[:], offs)
+        load_rows_by_four(nc, q_raw, query)
         nc.sync.dma_start(pages[:], offs2)
         nc.sync.dma_start(out=ptab_sb[:], in_=ptab)
         load_scale_rows(nc, k_scales, keys_scales)
@@ -73,52 +102,45 @@ def tile_attend_bpagetemper_kernel(tc, query, keys_words, keys_scales, ptab, gou
 
         q_codes = work.tile([P, Q], U32, name="q_codes", align_bytes=64)
         q_scales = work.tile([P, Q], U8, name="q_scales", align_bytes=64)
-        nc.scalar.copy(out=q_grouped[:], in_=q_raw[:].rearrange("p j w -> p w j"))
-        nc.vector.quantize_mx(out=q_codes[:].bitcast(FP8X4), scales=q_scales[:], in_=q_grouped[:].rearrange("p w j -> p (w j)"))
-        g_raw = work.tile([P, PACK, Q], F32, name="g_raw", tag="q_then_g", align_bytes=64)
-        nc.sync.dma_start(out=g_raw[:], in_=gout.rearrange("(p j) w -> p j w", j=PACK))
+        round_and_group(nc, q_grouped, q_raw)
+        quantize(nc, q_codes, q_scales, q_grouped)
+        g_raw = work.tile([P, PACK, Q], F32, name="g_raw", tag="staging", align_bytes=64)
+        load_rows_by_four(nc, g_raw, gout)
 
-        def list_half(h):
-            return slots[:, h * LIST_COLS_HALF : (h + 1) * LIST_COLS_HALF]
-
-        def cols(h):
-            return slice(h * HALF, (h + 1) * HALF)
-
-        a_ps = []
+        a_banks = []
         for h in range(HALVES):
             kg_scales = work.tile([P, HALF], U8, name=f"kg_scales{h}", tag=f"after_a{h}", align_bytes=64)
             nc.vector.tensor_copy(out=kg_scales[:], in_=k_scales[:].indirect(list_half(h)))
             bank = psum.tile([P, HALF], F32, name=f"a{h}")
-            nc.tensor.matmul_mx(out=bank[:], lhsT=q_codes[:].bitcast(FP8X4), lhsT_scale=q_scales[:],
-                                rhs=kg_words[:, cols(h)].bitcast(FP4X4), rhs_scale=kg_scales[:], start=True, stop=True)
-            a_ps.append(bank)
+            product(nc, bank, q_codes, q_scales, kg_words[:, cols(h)], kg_scales[:])
+            a_banks.append(bank)
         v_words = work.tile([P, T], U16, name="v_words", tag="after_a0", align_bytes=64)
         nc.sync.dma_start(out=v_words[:].bitcast(I32), in_=vals_words[0].bitcast(I32))
 
         g_codes = work.tile([P, Q], U32, name="g_codes", align_bytes=64)
         g_scales = work.tile([P, Q], U8, name="g_scales", align_bytes=64)
-
         s = work.tile([P, I], F32, name="s")
         vg_scales = work.tile([P, I], U8, name="vg_scales", align_bytes=64)
         nc.vector.tensor_copy(out=vg_scales[:], in_=v_scales[:].indirect(slots[:]))
-        old_sb = work.tile([P, U], F32, name="old_sb", tag="vs_then_old", align_bytes=64)
+        old_sb = work.tile([P, U], F32, name="old_sb", tag="v_scales_then_old", align_bytes=64)
         nc.sync.dma_start(out=old_sb[:], in_=old)
+
         for h in range(HALVES):
             a_sb = work.tile([P, HALF], F32, name=f"a_sb{h}")
-            nc.scalar.copy(out=a_sb[:], in_=a_ps[h][:])
-            nc.gpsimd.tensor_tensor(
-                out=s[:, cols(h)].rearrange("p (g j) -> p g j", j=PAGE),
-                in0=a_sb[:].rearrange("p (g j) -> p g j", j=PAGE),
-                in1=tp[:, h * PAGES_HALF : (h + 1) * PAGES_HALF].unsqueeze(2).to_broadcast([P, PAGES_HALF, PAGE]),
-                op=ALU.mult)
+            nc.scalar.copy(out=a_sb[:], in_=a_banks[h][:])
+            tp_half = tp[:, h * PAGES_HALF : (h + 1) * PAGES_HALF]
+            nc.gpsimd.tensor_tensor(out=by_page(s[:, cols(h)]), in0=by_page(a_sb[:]),
+                                    in1=tp_half.unsqueeze(2).to_broadcast([P, PAGES_HALF, PAGE]), op=ALU.mult)
+
         g_grouped = work.tile([P, Q, PACK], BF16, name="g_grouped", align_bytes=64)
-        nc.scalar.copy(out=g_grouped[:], in_=g_raw[:].rearrange("p j w -> p w j"))
+        round_and_group(nc, g_grouped, g_raw)
         neg_max = work.tile([P, 1], F32, name="neg_max")
-        neg_max0 = work.tile([P, 1], F32, name="neg_max0", tag="q_then_g", align_bytes=64)
-        neg_s1 = work.tile([P, HALF], F32, name="neg_s1", tag="after_c1_b", align_bytes=64)
+        neg_max0 = work.tile([P, 1], F32, name="neg_max0", tag="staging", align_bytes=64)
+        neg_s1 = work.tile([P, HALF], F32, name="neg_s1", tag="after_c1", align_bytes=64)
         nc.vector.tensor_reduce(out=neg_max0[:], in_=s[:, cols(0)], axis=AX.X, op=ALU.max, negate=True)
-        nc.vector.quantize_mx(out=g_codes[:].bitcast(FP8X4), scales=g_scales[:], in_=g_grouped[:].rearrange("p w j -> p (w j)"))
-        nc.vector.tensor_scalar(out=neg_s1[:], in0=s[:, cols(1)], scalar1=-1.0, scalar2=neg_max0[:], op0=ALU.mult, op1=ALU.min, accum_out=neg_max[:])
+        quantize(nc, g_codes, g_scales, g_grouped)
+        nc.vector.tensor_scalar(out=neg_s1[:], in0=s[:, cols(1)], scalar1=-1.0, scalar2=neg_max0[:],
+                                op0=ALU.mult, op1=ALU.min, accum_out=neg_max[:])
 
         p = work.tile([P, I], F32, name="p")
         z = work.tile([P, 1], F32, name="z")
@@ -129,43 +151,50 @@ def tile_attend_bpagetemper_kernel(tc, query, keys_words, keys_scales, ptab, gou
             nc.gpsimd.tensor_tensor(out=sp[:, cols(h)], in0=s[:, cols(h)], in1=p[:, cols(h)], op=ALU.mult)
         nc.scalar.activation(out=z[:], in_=z_half[0][:], func=ACT.Identity, bias=z_half[1][:])
 
-        c_ps = []
+        c_banks = []
         for h in range(HALVES):
-            vg_words = work.tile([P, HALF], U16, name=f"vg_words{h}", tag=f"after_c{h}_b", align_bytes=64)
+            vg_words = work.tile([P, HALF], U16, name=f"vg_words{h}", tag=f"after_c{h}", align_bytes=64)
             nc.vector.tensor_copy(out=vg_words[:], in_=v_words[:].indirect(list_half(h)))
             bank = psum.tile([P, HALF], F32, name=f"c{h}")
-            nc.tensor.matmul_mx(out=bank[:], lhsT=g_codes[:].bitcast(FP8X4), lhsT_scale=g_scales[:],
-                                rhs=vg_words[:].bitcast(FP4X4), rhs_scale=vg_scales[:, cols(h)], start=True, stop=True)
-            c_ps.append(bank)
+            product(nc, bank, g_codes, g_scales, vg_words[:], vg_scales[:, cols(h)])
+            c_banks.append(bank)
 
         pc = work.tile([P, I], F32, name="pc")
-        pc_sum0 = work.tile([P, 1], F32, name="pc_sum0")
-        mean0 = work.tile([P, 1], F32, name="mean0")
+        neg_sum0 = work.tile([P, 1], F32, name="neg_sum0")
+        neg_mean0 = work.tile([P, 1], F32, name="neg_mean0")
         mean1 = work.tile([P, 1], F32, name="mean1")
-        rz = work.tile([P, 1], F32, name="rz", tag="after_c0_b", align_bytes=64)
-        nc.vector.scalar_tensor_tensor(out=pc[:, cols(0)], in0=c_ps[0][:], scalar=1.0, in1=p[:, cols(0)],
-                                       op0=ALU.mult, op1=ALU.mult, accum_out=pc_sum0[:])
+        neg_mean = work.tile([P, 1], F32, name="neg_mean")
+        rz = work.tile([P, 1], F32, name="rz", tag="after_c0", align_bytes=64)
+        nc.vector.scalar_tensor_tensor(out=pc[:, cols(0)], in0=c_banks[0][:], scalar=-1.0, in1=p[:, cols(0)],
+                                       op0=ALU.mult, op1=ALU.mult, accum_out=neg_sum0[:])
         nc.vector.reciprocal(out=rz[:], in_=z[:])
-        nc.vector.scalar_tensor_tensor(out=pc[:, cols(1)], in0=c_ps[1][:], scalar=rz[:], in1=p[:, cols(1)],
+        nc.vector.scalar_tensor_tensor(out=pc[:, cols(1)], in0=c_banks[1][:], scalar=rz[:], in1=p[:, cols(1)],
                                        op0=ALU.mult, op1=ALU.mult, accum_out=mean1[:])
-        nc.scalar.activation(out=mean0[:], in_=pc_sum0[:], func=ACT.Copy, scale=rz[:])
-        shifted = work.tile([P, I], F32, name="shifted")
-        for h in range(HALVES):
-            nc.scalar.activation(out=shifted[:, cols(h)], in_=c_ps[h][:], func=ACT.Identity, scale=-1.0, bias=mean0[:])
+        nc.scalar.activation(out=neg_mean0[:], in_=neg_sum0[:], func=ACT.Copy, scale=rz[:])
+
+        on_vector, on_gpsimd = slice(0, VECTOR_SLOTS), slice(VECTOR_SLOTS, HALF)
+        c_less_mean0 = work.tile([P, VECTOR_SLOTS], F32, name="c_less_mean0")
+        c_less_mean = work.tile([P, GPSIMD_SLOTS], F32, name="c_less_mean")
+        w = work.tile([P, I], F32, name="w")
+        nc.scalar.activation(out=c_less_mean0[:], in_=c_banks[0][:, on_vector], func=ACT.Identity, bias=neg_mean0[:])
+        nc.scalar.activation(out=neg_mean[:], in_=mean1[:], func=ACT.Identity, scale=-1.0, bias=neg_mean0[:])
+        nc.scalar.activation(out=c_less_mean[:], in_=c_banks[0][:, on_gpsimd], func=ACT.Identity, bias=neg_mean[:])
+        nc.gpsimd.tensor_tensor(out=w[:, on_gpsimd], in0=c_less_mean[:], in1=sp[:, on_gpsimd], op=ALU.mult)
+        nc.vector.scalar_tensor_tensor(out=w[:, on_vector], in0=c_less_mean0[:], scalar=mean1[:], in1=sp[:, on_vector],
+                                       op0=ALU.subtract, op1=ALU.mult)
+        nc.vector.scalar_tensor_tensor(out=w[:, cols(1)], in0=c_banks[1][:], scalar=neg_mean[:], in1=sp[:, cols(1)],
+                                       op0=ALU.add, op1=ALU.mult)
+
+        page_sums = work.tile([P, G], F32, name="page_sums")
         factor = work.tile([P, G], F32, name="factor")
         nc.scalar.activation(out=factor[:], in_=sixty_four[:], func=ACT.Copy, scale=rz[:])
-
-        w = work.tile([P, I], F32, name="w")
-        page_sums = work.tile([P, G], F32, name="page_sums")
-        for h in range(HALVES):
-            nc.vector.scalar_tensor_tensor(out=w[:, cols(h)], in0=shifted[:, cols(h)], scalar=mean1[:], in1=sp[:, cols(h)],
-                                           op0=ALU.add, op1=ALU.mult)
-        for h in range(HALVES):
-            nc.vector.tensor_reduce(out=page_sums[:, h * PAGES_HALF : (h + 1) * PAGES_HALF],
-                                    in_=w[:, cols(h)].rearrange("p (g j) -> p g j", j=PAGE), axis=AX.X, op=ALU.add)
+        for part in (on_vector, cols(1), on_gpsimd):
+            nc.vector.tensor_reduce(out=page_sums[:, part.start // PAGE : part.stop // PAGE], in_=by_page(w[:, part]),
+                                    axis=AX.X, op=ALU.add)
         nc.vector.tensor_tensor(out=gf[:].indirect(pages[:]), in0=page_sums[:], in1=factor[:], op=ALU.mult)
+
         result = work.tile([P, U], F32, name="result")
-        for h in range(2):
-            half = slice(h * U // 2, (h + 1) * U // 2)
-            nc.vector.tensor_tensor(out=result[:, half], in0=gf[:, half], in1=old_sb[:, half], op=ALU.add)
-            nc.sync.dma_start(out=out[:, half], in_=result[:, half])
+        for first in range(0, U, U // 2):
+            part = slice(first, first + U // 2)
+            nc.vector.tensor_tensor(out=result[:, part], in0=gf[:, part], in1=old_sb[:, part], op=ALU.add)
+            nc.sync.dma_start(out=out[:, part], in_=result[:, part])

from contextlib import ExitStack

import concourse.mybir as mybir

D, T, I, G, U, Q = 512, 4096, 1024, 64, 512, 128
P = 128
PACK = 4
PAGE = I // G
HALF = 512
HALVES = I // HALF
PAGES_HALF = HALF // PAGE
LIST_COLS_HALF = HALF // 16
GPSIMD_SLOTS = 256
VECTOR_SLOTS = HALF - GPSIMD_SLOTS

F32 = mybir.dt.float32
BF16 = mybir.dt.bfloat16
I32 = mybir.dt.int32
U32 = mybir.dt.uint32
U16 = mybir.dt.uint16
U8 = mybir.dt.uint8
FP8X4 = mybir.dt.float8_e4m3fn_x4
FP4X4 = mybir.dt.float4_e2m1fn_x4
ALU = mybir.AluOpType
ACT = mybir.ActivationFunctionType
AX = mybir.AxisListType

FLOPS = 2 * 2 * D * Q * I


def load_scale_rows(nc, scale_tile, scales):
    rows = scales[0].rearrange("(quad r) c -> r quad c", r=4)
    for r in range(4):
        nc.sync.dma_start(out=scale_tile[r:P:32, :].bitcast(I32), in_=rows[r].bitcast(I32))


def load_rows_by_four(nc, raw, x):
    nc.sync.dma_start(out=raw[:], in_=x.rearrange("(p t) w -> p t w", t=PACK))


def round_and_group(nc, grouped, raw):
    nc.scalar.copy(out=grouped[:], in_=raw[:].rearrange("p t w -> p w t"))


def quantize(nc, codes, scales, grouped):
    nc.vector.quantize_mx(out=codes[:].bitcast(FP8X4), scales=scales[:], in_=grouped[:].rearrange("p w t -> p (w t)"))


def product(nc, bank, codes, scales, words, word_scales):
    nc.tensor.matmul_mx(out=bank[:], lhsT=codes[:].bitcast(FP8X4), lhsT_scale=scales[:],
                        rhs=words.bitcast(FP4X4), rhs_scale=word_scales, start=True, stop=True)


def by_page(ap):
    return ap.rearrange("p (g j) -> p g j", j=PAGE)


def cols(h):
    return slice(h * HALF, (h + 1) * HALF)


def tile_attend_bpagetemper_kernel(tc, query, keys_words, keys_scales, ptab, gout, vals_words, vals_scales, old, offs, offs2, out):
    nc = tc.nc
    with ExitStack() as ctx:
        held = ctx.enter_context(tc.tile_pool(name="held", bufs=1))
        work = ctx.enter_context(tc.tile_pool(name="work", bufs=1))
        psum = ctx.enter_context(tc.psum_pool(name="psum", bufs=1))

        slots = held.tile([P, I // 16], U16, name="slots")
        pages = held.tile([P, G // 16], U16, name="pages")
        k_scales = work.tile([P, T], U8, name="k_scales", align_bytes=64)
        q_raw = work.tile([P, PACK, Q], F32, name="q_raw", align_bytes=64)
        ptab_sb = work.tile([P, U], F32, name="ptab_sb", align_bytes=64)
        gf = held.tile([P, U], F32, name="gf")
        k_words = work.tile([P, T], U16, name="k_words", align_bytes=64)
        q_grouped = work.tile([P, Q, PACK], BF16, name="q_grouped", tag="staging", align_bytes=64)
        v_scales = work.tile([P, T], U8, name="v_scales", tag="v_scales_then_old", align_bytes=64)
        sixty_four = work.tile([P, G], F32, name="sixty_four")

        def list_half(h):
            return slots[:, h * LIST_COLS_HALF : (h + 1) * LIST_COLS_HALF]

        nc.vector.memset(k_scales[:].bitcast(I32), 0)
        nc.vector.memset(v_scales[:].bitcast(I32), 0)
        nc.vector.memset(gf[:], 0.0)
        nc.vector.memset(sixty_four[:], 64.0)

        nc.sync.dma_start(out=k_words[:].bitcast(I32), in_=keys_words[0].bitcast(I32))
        nc.sync.dma_start(slots[:], offs)
        load_rows_by_four(nc, q_raw, query)
        nc.sync.dma_start(pages[:], offs2)
        nc.sync.dma_start(out=ptab_sb[:], in_=ptab)
        load_scale_rows(nc, k_scales, keys_scales)
        load_scale_rows(nc, v_scales, vals_scales)

        kg_words = work.tile([P, I], U16, name="kg_words", align_bytes=64)
        nc.vector.tensor_copy(out=kg_words[:], in_=k_words[:].indirect(slots[:]))
        ptab_g = work.tile([P, G], F32, name="ptab_g")
        tp = work.tile([P, G], F32, name="tp")
        nc.vector.tensor_copy(out=ptab_g[:], in_=ptab_sb[:].indirect(pages[:]))
        nc.scalar.activation(out=tp[:], in_=ptab_g[:], func=ACT.Exp)

        q_codes = work.tile([P, Q], U32, name="q_codes", align_bytes=64)
        q_scales = work.tile([P, Q], U8, name="q_scales", align_bytes=64)
        round_and_group(nc, q_grouped, q_raw)
        quantize(nc, q_codes, q_scales, q_grouped)
        g_raw = work.tile([P, PACK, Q], F32, name="g_raw", tag="staging", align_bytes=64)
        load_rows_by_four(nc, g_raw, gout)

        a_banks = []
        for h in range(HALVES):
            kg_scales = work.tile([P, HALF], U8, name=f"kg_scales{h}", tag=f"after_a{h}", align_bytes=64)
            nc.vector.tensor_copy(out=kg_scales[:], in_=k_scales[:].indirect(list_half(h)))
            bank = psum.tile([P, HALF], F32, name=f"a{h}")
            product(nc, bank, q_codes, q_scales, kg_words[:, cols(h)], kg_scales[:])
            a_banks.append(bank)
        v_words = work.tile([P, T], U16, name="v_words", tag="after_a0", align_bytes=64)
        nc.sync.dma_start(out=v_words[:].bitcast(I32), in_=vals_words[0].bitcast(I32))

        g_codes = work.tile([P, Q], U32, name="g_codes", align_bytes=64)
        g_scales = work.tile([P, Q], U8, name="g_scales", align_bytes=64)
        s = work.tile([P, I], F32, name="s")
        vg_scales = work.tile([P, I], U8, name="vg_scales", align_bytes=64)
        nc.vector.tensor_copy(out=vg_scales[:], in_=v_scales[:].indirect(slots[:]))
        old_sb = work.tile([P, U], F32, name="old_sb", tag="v_scales_then_old", align_bytes=64)
        nc.sync.dma_start(out=old_sb[:], in_=old)

        for h in range(HALVES):
            a_sb = work.tile([P, HALF], F32, name=f"a_sb{h}")
            nc.scalar.copy(out=a_sb[:], in_=a_banks[h][:])
            tp_half = tp[:, h * PAGES_HALF : (h + 1) * PAGES_HALF]
            nc.gpsimd.tensor_tensor(out=by_page(s[:, cols(h)]), in0=by_page(a_sb[:]),
                                    in1=tp_half.unsqueeze(2).to_broadcast([P, PAGES_HALF, PAGE]), op=ALU.mult)

        g_grouped = work.tile([P, Q, PACK], BF16, name="g_grouped", align_bytes=64)
        round_and_group(nc, g_grouped, g_raw)
        neg_max = work.tile([P, 1], F32, name="neg_max")
        neg_max0 = work.tile([P, 1], F32, name="neg_max0", tag="staging", align_bytes=64)
        neg_s1 = work.tile([P, HALF], F32, name="neg_s1", tag="after_c1", align_bytes=64)
        nc.vector.tensor_reduce(out=neg_max0[:], in_=s[:, cols(0)], axis=AX.X, op=ALU.max, negate=True)
        quantize(nc, g_codes, g_scales, g_grouped)
        nc.vector.tensor_scalar(out=neg_s1[:], in0=s[:, cols(1)], scalar1=-1.0, scalar2=neg_max0[:],
                                op0=ALU.mult, op1=ALU.min, accum_out=neg_max[:])

        p = work.tile([P, I], F32, name="p")
        z = work.tile([P, 1], F32, name="z")
        z_half = [work.tile([P, 1], F32, name=f"z_half{h}") for h in range(HALVES)]
        sp = work.tile([P, I], F32, name="sp")
        for h in range(HALVES):
            nc.scalar.activation(out=p[:, cols(h)], in_=s[:, cols(h)], func=ACT.Exp, bias=neg_max[:], accum_out=z_half[h][:])
            nc.gpsimd.tensor_tensor(out=sp[:, cols(h)], in0=s[:, cols(h)], in1=p[:, cols(h)], op=ALU.mult)
        nc.scalar.activation(out=z[:], in_=z_half[0][:], func=ACT.Identity, bias=z_half[1][:])

        c_banks = []
        for h in range(HALVES):
            vg_words = work.tile([P, HALF], U16, name=f"vg_words{h}", tag=f"after_c{h}", align_bytes=64)
            nc.vector.tensor_copy(out=vg_words[:], in_=v_words[:].indirect(list_half(h)))
            bank = psum.tile([P, HALF], F32, name=f"c{h}")
            product(nc, bank, g_codes, g_scales, vg_words[:], vg_scales[:, cols(h)])
            c_banks.append(bank)

        pc = work.tile([P, I], F32, name="pc")
        neg_sum0 = work.tile([P, 1], F32, name="neg_sum0")
        neg_mean0 = work.tile([P, 1], F32, name="neg_mean0")
        mean1 = work.tile([P, 1], F32, name="mean1")
        neg_mean = work.tile([P, 1], F32, name="neg_mean")
        rz = work.tile([P, 1], F32, name="rz", tag="after_c0", align_bytes=64)
        nc.vector.scalar_tensor_tensor(out=pc[:, cols(0)], in0=c_banks[0][:], scalar=-1.0, in1=p[:, cols(0)],
                                       op0=ALU.mult, op1=ALU.mult, accum_out=neg_sum0[:])
        nc.vector.reciprocal(out=rz[:], in_=z[:])
        nc.vector.scalar_tensor_tensor(out=pc[:, cols(1)], in0=c_banks[1][:], scalar=rz[:], in1=p[:, cols(1)],
                                       op0=ALU.mult, op1=ALU.mult, accum_out=mean1[:])
        nc.scalar.activation(out=neg_mean0[:], in_=neg_sum0[:], func=ACT.Copy, scale=rz[:])

        on_vector, on_gpsimd = slice(0, VECTOR_SLOTS), slice(VECTOR_SLOTS, HALF)
        c_less_mean0 = work.tile([P, VECTOR_SLOTS], F32, name="c_less_mean0")
        c_less_mean = work.tile([P, GPSIMD_SLOTS], F32, name="c_less_mean")
        w = work.tile([P, I], F32, name="w")
        nc.scalar.activation(out=c_less_mean0[:], in_=c_banks[0][:, on_vector], func=ACT.Identity, bias=neg_mean0[:])
        nc.scalar.activation(out=neg_mean[:], in_=mean1[:], func=ACT.Identity, scale=-1.0, bias=neg_mean0[:])
        nc.scalar.activation(out=c_less_mean[:], in_=c_banks[0][:, on_gpsimd], func=ACT.Identity, bias=neg_mean[:])
        nc.gpsimd.tensor_tensor(out=w[:, on_gpsimd], in0=c_less_mean[:], in1=sp[:, on_gpsimd], op=ALU.mult)
        nc.vector.scalar_tensor_tensor(out=w[:, on_vector], in0=c_less_mean0[:], scalar=mean1[:], in1=sp[:, on_vector],
                                       op0=ALU.subtract, op1=ALU.mult)
        nc.vector.scalar_tensor_tensor(out=w[:, cols(1)], in0=c_banks[1][:], scalar=neg_mean[:], in1=sp[:, cols(1)],
                                       op0=ALU.add, op1=ALU.mult)

        page_sums = work.tile([P, G], F32, name="page_sums")
        factor = work.tile([P, G], F32, name="factor")
        nc.scalar.activation(out=factor[:], in_=sixty_four[:], func=ACT.Copy, scale=rz[:])
        for part in (on_vector, cols(1), on_gpsimd):
            nc.vector.tensor_reduce(out=page_sums[:, part.start // PAGE : part.stop // PAGE], in_=by_page(w[:, part]),
                                    axis=AX.X, op=ALU.add)
        nc.vector.tensor_tensor(out=gf[:].indirect(pages[:]), in0=page_sums[:], in1=factor[:], op=ALU.mult)

        result = work.tile([P, U], F32, name="result")
        for first in range(0, U, U // 2):
            part = slice(first, first + U // 2)
            nc.vector.tensor_tensor(out=result[:, part], in0=gf[:, part], in1=old_sb[:, part], op=ALU.add)
            nc.sync.dma_start(out=out[:, part], in_=result[:, part])
